import numpy as np
import ml_dtypes


def mxq(x, axis, fmt="e4m3"):
    dtype, down = {"e4m3": (ml_dtypes.float8_e4m3fn, 7), "e5m2": (ml_dtypes.float8_e5m2, 14)}[fmt]
    v = np.moveaxis(np.asarray(x, np.float32).astype(ml_dtypes.bfloat16).astype(np.float64), axis, -1)
    blocks = v.reshape(v.shape[:-1] + (-1, 32))
    amax = np.abs(blocks).max(-1, keepdims=True)
    byte = np.maximum(np.where(amax > 0, np.frexp(amax)[1] - 1 + 127, 0) - down, 1)
    scale = np.exp2(byte - 127.0)
    codes = (blocks / scale).astype(np.float32).astype(dtype).astype(np.float64)
    return np.moveaxis((codes * scale).reshape(v.shape), -1, axis)


WIDE = False


def mx_kscale(k, group=512):
    if not WIDE:
        return np.ones(k)
    levels = np.array([10, -10, 5, -5, 0])
    if group != 512:
        return np.exp2(np.random.permutation(np.resize(levels, k // group))).repeat(group)
    if k % 512:
        return np.exp2(np.random.permutation(np.resize(levels, k // 32))).repeat(32)
    a = np.empty((k // 512, 16))
    for p in range(k // 512):
        a[p, :8] = np.random.permutation(np.resize(levels, 8))
        for g in range(8):
            far = levels[np.abs(levels - a[p, g]) >= 10]
            a[p, g + 8] = far[np.random.randint(len(far))]
    return np.exp2(a.ravel()).repeat(32)


def f64(x):
    return np.asarray(x).astype(np.float64)


def striped(idx):
    return np.tile(np.asarray(idx).reshape(-1, 16).T, (8, 1)).astype(np.uint16)


def unstriped(offs):
    return offs[:16].T.reshape(-1).astype(np.int64)


H, KV, D, NQ, N = 8, 2, 128, 512, 512


def setup_inputs():
    n = np.random.standard_normal
    s = mx_kscale(D, 0)[:, None]
    u = mx_kscale(N)
    t = np.random.uniform(0.5, 2.0, N) * u
    v = n((KV, N, 128))
    return {
        "qT": (n((H, D, NQ)) * s * (0.70 / np.sqrt(D))).astype(np.float32),
        "kT": (n((KV, D, N)) / s).astype(np.float32),
        "t": t.reshape(N, 1).astype(np.float32),
        "v": (v / t[:, None]).astype(np.float32),
        "kb": (0.5 * n((N, 1))).astype(np.float32),
        "gn": np.tile(np.random.uniform(0.5, 2.0, 128), (128, 1)).astype(np.float32),
        "og": n((H, NQ, 128)).astype(np.float32),
    }


def reference(qT, kT, t, v, kb, gn, og):
    a = np.repeat(mxq(f64(kT), 1, "e4m3"), H // KV, 0).transpose(0, 2, 1) @ mxq(f64(qT), 1, "e4m3")
    a = a + f64(kb)
    p = np.maximum(a, 0.0)
    w = p * f64(t)
    y = mxq(w, 1, "e4m3").transpose(0, 2, 1) @ np.repeat(mxq(f64(v), 1, "e4m3"), H // KV, 0)
    y = y / 16.0
    y = y / np.sqrt(np.mean(np.square(y), -1, keepdims=True) + 1e-5) * f64(gn)[:1]
    y = y / (1.0 + np.exp(-f64(og)))
    return y

@@ -1,0 +1,233 @@
+from contextlib import ExitStack
+
+import concourse.mybir as mybir
+
+H, KV, D, NQ, N = 8, 2, 128, 512, 512
+FLOPS = 2 * 2 * H * NQ * N * D
+
+F32 = mybir.dt.float32
+BF16 = mybir.dt.bfloat16
+U32 = mybir.dt.uint32
+U8 = mybir.dt.uint8
+X4 = mybir.dt.float8_e4m3fn_x4
+ALU = mybir.AluOpType
+ACT = mybir.ActivationFunctionType
+
+P = 128
+HEADS = ((2, 3, 4, 5), (0, 1, 6, 7))
+ORDER = ["dk","dt","dqA0","dv","ik2","ik3","ik0","ik1","dqA1","cst","iqA0b","iqA0a","zk1","zk0","zqA0","dog1","iv","ma2","ma1","dog3","sa2","iqA1a","ma3","zv","ma0","iqA1b","sa1","dqB1","mb2","sig1","sa0","mb1","zqA1","mb0","sb2","dqB0","g2","sig3","iw2","ma6","dog2","g3","sb0","zw2","sa3","g6","dog0","y2","ma4","iw0","sb1","mb3","sa6","iqB0b","zw0","ma5","sa4","iw1","y0","sig2","mb6","iqB0a","zw1","mb4","zqB0","iqB1b","sig0","y1","g4","sb4","sb3","g1","ma8","sw","g0","ma7","iw3","sa8","sa7","zw3","mb8","sa5","iw4","mb7","ss0","g5","mb5","zw4","sb7","iqB1a","y3","g7","y4","rs0","ma11","ss1","fin0","sb5","iw7","st0","sb6","iw5","ma9","sb8","ma10","iw6","sa11","zw7","rs1","zw6","sa10","y7","fin1","y6","sa9","mb10","iw8","st1","ss3","mb9","zw5","zqB1","sb10","y5","zw8","ma12","sb9","ss2","y8","iw10","mb11","sa12","iw9","ma13","rs2","sb11","mb12","fin2","sa13","ma14","iw11","st2","sb12","ma15","zw9","rs3","zw11","mb13","sa14","iw12","y9","sa15","y11","fin3","mb14","sb13","zw12","mb15","st3","zw10","sb14","iw13","y12","y10","sb15","iw14","ss4","zw13","iw15","ss5","y13","zw14","rs4","zw15","rs5","ss6","y14","fin4","y15","fin5","rs6","ss7","st4","fin6","st5","rs7","fin7","st6","st7"]
+ON_ACT = ["ik2","ik1","iqA0a","iqA1a","iqA1b","sb2","sb0","sa3","sb1","sa6","sa4","sb3","sa7","sa5","sb7","sb5","sb6","sb8","sa11","sa10","sa9","sb10","sa12","sb11","sa13","sb12","sa14","sa15","sb13","sb14","sb15"]
+
+
+def tile_rows_a_relu_kb_onorm_gate_kernel(tc, qT, kT, t, v, kb, gn, og, out):
+    nc = tc.nc
+    with ExitStack() as ctx:
+        sb = ctx.enter_context(tc.tile_pool(name="sb", bufs=1))
+        ps = ctx.enter_context(tc.psum_pool(name="ps", bufs=1))
+
+        def tiles(pool, name, count, shape, dtype):
+            if pool is ps:
+                return [pool.tile(shape, dtype, name="%s%d" % (name, i)) for i in range(count)]
+            return [pool.tile(shape, dtype, name="%s%d" % (name, i), align_bytes=64) for i in range(count)]
+
+        (t_sb, kb_sb, sgn, tabs, tkb, ge0) = tiles(sb, "tok", 6, [P, 4], F32)
+        (warm_in, warm_out) = tiles(sb, "warm", 2, [P, 1], F32)
+        (gn_sb,) = tiles(sb, "gn", 1, [P, 128], F32)
+        (k_raw,) = tiles(sb, "k_raw", 1, [P, 4, N], F32)
+        (k_bf,) = tiles(sb, "k_bf", 1, [P, 4, 128, 4], BF16)
+        (k_codes,) = tiles(sb, "k_codes", 1, [P, N], U32)
+        (k_scales,) = tiles(sb, "k_scales", 1, [P, N], U8)
+        (v_raw,) = tiles(sb, "v_raw", 1, [P, KV, 4, 128], F32)
+        (v_bf,) = tiles(sb, "v_bf", 1, [P, KV, 128, 4], BF16)
+        (v_codes,) = tiles(sb, "v_codes", 1, [P, KV * 128], U32)
+        (v_scales,) = tiles(sb, "v_scales", 1, [P, KV * 128], U8)
+        q_raw = tiles(sb, "q_raw", 4, [P, 4, 256], F32)
+        q_bf = tiles(sb, "q_bf", 4, [P, 2, 128, 4], BF16)
+        q_codes = tiles(sb, "q_codes", 4, [P, 256], U32)
+        q_scales = tiles(sb, "q_scales", 4, [P, 256], U8)
+        og_sb = tiles(sb, "og_sb", 4, [P, 4, 256], F32)
+        sig = tiles(sb, "sig", 4, [P, 4, 256], F32)
+        gate = tiles(sb, "gate", 8, [P, 4, 128], F32)
+        w_rows = tiles(sb, "w_rows", 16, [P, 4, 256], BF16)
+        w_bf = tiles(sb, "w_bf", 16, [P, 256, 4], BF16)
+        w_codes = tiles(sb, "w_codes", 16, [P, 256], U32)
+        w_scales = tiles(sb, "w_scales", 16, [P, 256], U8)
+        squares = tiles(sb, "squares", 8, [P, 4, 128], BF16)
+        ssq = tiles(sb, "ssq", 8, [P, 4], F32)
+        rstd = tiles(sb, "rstd", 8, [P, 4], F32)
+        res = tiles(sb, "res", 8, [P, 4, 128], F32)
+        score = tiles(ps, "score", 4, [P, 2, 256], F32)
+        ybank = tiles(ps, "ybank", 4, [P, 4, 128], F32)
+
+        def quantize(codes, scales, src):
+            nc.vector.quantize_mx(out=codes.bitcast(X4), scales=scales, in_=src)
+
+        def cast(name, dst, src):
+            if name in ON_ACT:
+                nc.scalar.copy(out=dst, in_=src)
+            else:
+                nc.vector.tensor_copy(out=dst, in_=src)
+
+        def runs(c):
+            return ((0, 2, 4),) if c < 2 else ((0, 0, 2), (2, 6, 2))
+
+        def load_q(c):
+            cols = slice(256 * (c % 2), 256 * (c % 2) + 256)
+            for g0, h0, nh in runs(c):
+                nc.sync.dma_start(out=q_raw[c][32 * g0 : 32 * (g0 + nh)],
+                                  in_=qT[h0 : h0 + nh, :, cols].rearrange("h (p j) n -> (h p) j n", j=4))
+
+        def load_og(c):
+            rows = slice(256 * (c % 2), 256 * (c % 2) + 256)
+            for g0, h0, nh in runs(c):
+                nc.sync.dma_start(out=og_sb[c][:, g0 : g0 + nh, :],
+                                  in_=og[h0 : h0 + nh, rows, :].rearrange("h (m u) e -> m h (u e)", u=2))
+
+        QN = ("qA0", "qA1", "qB0", "qB1")
+
+        def dt():
+            nc.scalar.dma_start(out=t_sb[:], in_=t.rearrange("(p r) o -> p (r o)", r=4))
+            nc.scalar.dma_start(out=kb_sb[:], in_=kb.rearrange("(p r) o -> p (r o)", r=4))
+            nc.scalar.dma_start(out=gn_sb[:], in_=gn)
+            nc.vector.memset(warm_in[:], 0.0)
+            nc.scalar.activation(out=warm_out[:], in_=warm_in[:], func=ACT.Sigmoid)
+
+        def dk():
+            rows = kT.rearrange("k (p j) n -> (k p) j n", j=4)
+            nc.sync.dma_start(out=k_raw[32:96], in_=rows)
+            nc.scalar.dma_start(out=k_raw[96:128], in_=rows[32:64])
+            nc.sync.dma_start(out=k_raw[0:32], in_=rows[0:32])
+
+        def dv():
+            nc.sync.dma_start(out=v_raw[:].rearrange("p k j e -> p k (j e)"),
+                              in_=v.rearrange("k (p j) e -> p k (j e)", j=4))
+
+        def cst():
+            nc.vector.tensor_scalar(ge0[:], t_sb[:], 0.0, 2.0, ALU.is_ge, ALU.mult)
+            nc.vector.tensor_scalar(sgn[:], ge0[:], -1.0, None, ALU.add)
+            nc.vector.tensor_tensor(tabs[:], t_sb[:], sgn[:], ALU.mult)
+            nc.vector.tensor_tensor(tkb[:], tabs[:], kb_sb[:], ALU.mult)
+
+        def ik(j):
+            cast("ik%d" % j, k_bf[:, :, 32 * j : 32 * j + 32, :].rearrange("p r s j -> p s r j"),
+                 k_raw[:, :, 128 * j : 128 * j + 128].rearrange("p j (s r) -> p s r j", r=4))
+
+        def zk(x):
+            quantize(k_codes[:, 256 * x : 256 * x + 256], k_scales[:, 256 * x : 256 * x + 256],
+                     k_bf[:, 2 * x : 2 * x + 2].rearrange("p r s j -> p (r s j)"))
+
+        def iq(c, x):
+            cast("i" + QN[c] + "ab"[x], q_bf[c][:, :, 64 * x : 64 * x + 64, :].rearrange("p u m j -> p m u j"),
+                 q_raw[c][:, :, 128 * x : 128 * x + 128].rearrange("p j (m u) -> p m u j", u=2))
+
+        def zq(c):
+            quantize(q_codes[c][:], q_scales[c][:], q_bf[c][:].rearrange("p u m j -> p (u m j)"))
+
+        def iv():
+            nc.vector.tensor_tensor(v_bf[:], v_raw[:].rearrange("p k j e -> p k e j"),
+                                    sgn[:].unsqueeze(1).unsqueeze(1).broadcast_to([P, KV, 128, 4]), ALU.mult)
+
+        def zv():
+            quantize(v_codes[:], v_scales[:], v_bf[:].rearrange("p k e j -> p (k e j)"))
+
+        def mm(n, part):
+            g, c = n % 4, n // 4
+            rows = slice(32 * g, 32 * g + 32)
+            for rr in range(2):
+                kc = slice(128 * (2 * part + rr), 128 * (2 * part + rr) + 128)
+                for u in range(2):
+                    qc = slice(128 * u, 128 * u + 128)
+                    nc.tensor.matmul_mx(out=score[g][:, rr, qc], lhsT=k_codes[rows, kc].bitcast(X4),
+                                        lhsT_scale=k_scales[rows, kc], rhs=q_codes[c][rows, qc].bitcast(X4),
+                                        rhs_scale=q_scales[c][rows, qc], start=True, stop=True)
+
+        def s1(n, part):
+            g = n % 4
+            for rr in range(2):
+                r = 2 * part + rr
+                if "s%s%d" % ("ab"[part], n) in ON_ACT:
+                    nc.scalar.activation(out=w_rows[n][:, r, :], in_=score[g][:, rr, :], func=ACT.Relu,
+                                         bias=tkb[:, r : r + 1], scale=tabs[:, r : r + 1])
+                else:
+                    nc.vector.tensor_scalar(w_rows[n][:, r, :], score[g][:, rr, :], kb_sb[:, r : r + 1],
+                                            tabs[:, r : r + 1], ALU.add, ALU.mult)
+
+        def iw(n):
+            dst = w_bf[n][:].rearrange("p (c i) r -> p c r i", i=4)
+            src = w_rows[n][:].rearrange("p r (c i) -> p c r i", i=4)
+            if "iw%d" % n in ON_ACT:
+                nc.scalar.activation(out=dst, in_=src, func=ACT.Relu)
+            else:
+                nc.vector.tensor_scalar(dst, src, 0.0, None, ALU.max)
+
+        def zw(n):
+            quantize(w_codes[n][:], w_scales[n][:], w_bf[n][:].rearrange("p q r -> p (q r)"))
+
+        def ymm(n):
+            kv = (n % 4) // 2
+            vc = slice(128 * kv, 128 * kv + 128)
+            for u in range(2):
+                qc = slice(128 * u, 128 * u + 128)
+                nc.tensor.matmul_mx(out=ybank[(n // 2) % 4][:, 2 * (n % 2) + u, :], lhsT=w_codes[n][:, qc].bitcast(X4),
+                                    lhsT_scale=w_scales[n][:, qc], rhs=v_codes[:, vc].bitcast(X4),
+                                    rhs_scale=v_scales[:, vc], start=True, stop=True)
+
+        def sg(c):
+            nc.scalar.activation(out=sig[c][:], in_=og_sb[c][:], func=ACT.Sigmoid)
+
+        def g2(p):
+            g0 = 2 * (p % 2)
+            nc.vector.tensor_tensor(gate[p][:], sig[p // 2][:, g0 : g0 + 2, :].rearrange("p g (u e) -> p (g u) e", u=2),
+                                    gn_sb[:].unsqueeze(1).broadcast_to([P, 4, 128]), ALU.mult)
+
+        def ss(p):
+            for i in range(4):
+                nc.scalar.activation(out=squares[p][:, i, :], in_=ybank[p % 4][:, i, :], func=ACT.Square,
+                                     accum_out=ssq[p][:, i : i + 1])
+
+        def rs(p):
+            nc.scalar.activation(out=rstd[p][:], in_=ssq[p][:], func=ACT.Abs_reciprocal_sqrt,
+                                 scale=1.0 / 128.0, bias=256.0 * 1e-5)
+
+        def fin(p):
+            for i in range(4):
+                nc.vector.scalar_tensor_tensor(res[p][:, i, :], ybank[p % 4][:, i, :], rstd[p][:, i : i + 1],
+                                               gate[p][:, i, :], ALU.mult, ALU.mult)
+
+        def st(p):
+            c = p // 2
+            h0 = HEADS[c // 2][2 * (p % 2)]
+            rows = slice(256 * (c % 2), 256 * (c % 2) + 256)
+            nc.sync.dma_start(out=out[h0 : h0 + 2, rows, :].rearrange("h (m u) e -> m h (u e)", u=2),
+                              in_=res[p][:].rearrange("p (g u) e -> p g (u e)", u=2))
+
+        def bind(f, *a):
+            return lambda: f(*a)
+
+        task = {"dt": dt, "dk": dk, "dv": dv, "cst": cst, "iv": iv, "zv": zv, "sw": lambda: None}
+        for c in range(4):
+            task["d" + QN[c]] = bind(load_q, c)
+            task["dog%d" % c] = bind(load_og, c)
+            task["ik%d" % c] = bind(ik, c)
+            task["i" + QN[c] + "a"] = bind(iq, c, 0)
+            task["i" + QN[c] + "b"] = bind(iq, c, 1)
+            task["z" + QN[c]] = bind(zq, c)
+            task["sig%d" % c] = bind(sg, c)
+        for x in range(2):
+            task["zk%d" % x] = bind(zk, x)
+        for n in range(16):
+            for part in range(2):
+                task["m%s%d" % ("ab"[part], n)] = bind(mm, n, part)
+                task["s%s%d" % ("ab"[part], n)] = bind(s1, n, part)
+            task["iw%d" % n] = bind(iw, n)
+            task["zw%d" % n] = bind(zw, n)
+            task["y%d" % n] = bind(ymm, n)
+        for p in range(8):
+            task["g%d" % p] = bind(g2, p)
+            task["ss%d" % p] = bind(ss, p)
+            task["rs%d" % p] = bind(rs, p)
+            task["fin%d" % p] = bind(fin, p)
+            task["st%d" % p] = bind(st, p)
+        with tc.manual_schedule():
+            for name in ORDER:
+                task[name]()

@@ -15,8 +15,11 @@ ACT = mybir.ActivationFunctionType
 
 P = 128
 HEADS = ((2, 3, 4, 5), (0, 1, 6, 7))
-ORDER = ["dk","dt","dqA0","dv","ik2","ik3","ik0","ik1","dqA1","cst","iqA0b","iqA0a","zk1","zk0","zqA0","dog1","iv","ma2","ma1","dog3","sa2","iqA1a","ma3","zv","ma0","iqA1b","sa1","dqB1","mb2","sig1","sa0","mb1","zqA1","mb0","sb2","dqB0","g2","sig3","iw2","ma6","dog2","g3","sb0","zw2","sa3","g6","dog0","y2","ma4","iw0","sb1","mb3","sa6","iqB0b","zw0","ma5","sa4","iw1","y0","sig2","mb6","iqB0a","zw1","mb4","zqB0","iqB1b","sig0","y1","g4","sb4","sb3","g1","ma8","sw","g0","ma7","iw3","sa8","sa7","zw3","mb8","sa5","iw4","mb7","ss0","g5","mb5","zw4","sb7","iqB1a","y3","g7","y4","rs0","ma11","ss1","fin0","sb5","iw7","st0","sb6","iw5","ma9","sb8","ma10","iw6","sa11","zw7","rs1","zw6","sa10","y7","fin1","y6","sa9","mb10","iw8","st1","ss3","mb9","zw5","zqB1","sb10","y5","zw8","ma12","sb9","ss2","y8","iw10","mb11","sa12","iw9","ma13","rs2","sb11","mb12","fin2","sa13","ma14","iw11","st2","sb12","ma15","zw9","rs3","zw11","mb13","sa14","iw12","y9","sa15","y11","fin3","mb14","sb13","zw12","mb15","st3","zw10","sb14","iw13","y12","y10","sb15","iw14","ss4","zw13","iw15","ss5","y13","zw14","rs4","zw15","rs5","ss6","y14","fin4","y15","fin5","rs6","ss7","st4","fin6","st5","rs7","fin7","st6","st7"]
-ON_ACT = ["ik2","ik1","iqA0a","iqA1a","iqA1b","sb2","sb0","sa3","sb1","sa6","sa4","sb3","sa7","sa5","sb7","sb5","sb6","sb8","sa11","sa10","sa9","sb10","sa12","sb11","sa13","sb12","sa14","sa15","sb13","sb14","sb15"]
+ORDER = ["dk","dt","dqA0","ik0","dog0","ik2","ik3","ik1","zk0","iqA0a","xqB0","dv","iqA0b","zqA0","dqB0","zk1","cst","sig0","m0_0","m1_0","dqA1","iv","s0_0","m2_0","s1_0","m3_0","g0","s2_0","dog1","m0_1","iqB0a","m1_1","s3_0","zv","iqB0b","m2_1","s0_1","iqA1a","dog3","iqA1b","m3_1","s1_1","zqB0","zqA1","s2_1","xqB1","g1","dqB1","m4_0","sig1","iw0","m6_0","iw2","dog2","m5_0","s4_0","zw0","s3_1","g3","m4_1","s5_0","sig3","iw1","m5_1","s4_1","iqB1a","m7_0","zw2","sig2","s6_0","m4_2","s5_1","m6_1","s7_0","g2","s4_2","m5_2","iw3","s6_1","m7_1","zw1","iqB1b","sw","m4_3","s5_2","g4","m5_3","zw3","s4_3","zqB1","m6_2","g5","s7_1","y1","iw4","s5_3","m7_2","s6_2","m9_0","g6","ss1","m6_3","iw5","s7_2","y0","rs1","s9_0","m7_3","zw4","s6_3","m8_0","zw5","ss0","m9_1","fin1","st1","s7_3","y2","iw6","rs0","s8_0","m10_0","ss2","y3","fin0","st0","m8_1","s10_0","zw6","m11_0","s9_1","iw7","y4","s8_1","m10_1","ss3","iw9","zw7","ss4","iw8","rs2","s10_1","y5","zw9","s11_0","fin2","st2","zw8","rs4","rs3","iw11","iw10","m12_0","ss5","fin4","st4","y6","zw11","s12_0","fin3","st3","y8","rs5","zw10","ss6","iw12","y7","fin5","st5","ss8","rs6","zw12","fin6","st6","ss7","y9","g7","rs7","rs8","ss9","fin7","st7","rs9","fin8","st8","fin9","st9"]
+ON_ACT = ["ik2","iqA0a","s0_0","s1_0","s2_0","s3_0","s0_1","s1_1","s2_1","s4_0","s3_1","s4_1","s7_0","s4_2","s6_1","s4_3","s7_1","s5_3","s6_2","s7_2","s9_0","s6_3","s7_3","s8_0","s10_0","s9_1","s8_1","s10_1","s11_0","iw11","s12_0"]
+UNITS = ([(g, [(0, 0), (0, 1)]) for g in range(4)] + [(g, [(1, 0), (1, 1), (2, 0), (2, 1)]) for g in range(4)]
+         + [(g, [(3, 0), (3, 1)]) for g in range(3)] + [(3, [(3, 0)]), (3, [(3, 1)])])
+GROUPS = [[0, 1], [2, 3], [4], [5], [6], [7], [8, 9], [10], [11], [12]]
 
 
 def tile_rows_a_relu_kb_onorm_gate_kernel(tc, qT, kT, t, v, kb, gn, og, out):
@@ -47,16 +50,17 @@ def tile_rows_a_relu_kb_onorm_gate_kernel(tc, qT, kT, t, v, kb, gn, og, out):
         q_scales = tiles(sb, "q_scales", 4, [P, 256], U8)
         og_sb = tiles(sb, "og_sb", 4, [P, 4, 256], F32)
         sig = tiles(sb, "sig", 4, [P, 4, 256], F32)
-        gate = tiles(sb, "gate", 8, [P, 4, 128], F32)
-        w_rows = tiles(sb, "w_rows", 16, [P, 4, 256], BF16)
-        w_bf = tiles(sb, "w_bf", 16, [P, 256, 4], BF16)
-        w_codes = tiles(sb, "w_codes", 16, [P, 256], U32)
-        w_scales = tiles(sb, "w_scales", 16, [P, 256], U8)
-        squares = tiles(sb, "squares", 8, [P, 4, 128], BF16)
-        ssq = tiles(sb, "ssq", 8, [P, 4], F32)
-        rstd = tiles(sb, "rstd", 8, [P, 4], F32)
-        res = tiles(sb, "res", 8, [P, 4, 128], F32)
-        score = tiles(ps, "score", 4, [P, 2, 256], F32)
+        gate = tiles(sb, "gate", 4, [P, 4, 256], F32)
+        widths = [128 * len(blocks) for g, blocks in UNITS]
+        w_rows = [tiles(sb, "w_rows%d_" % n, 1, [P, 4, w], BF16)[0] for n, w in enumerate(widths)]
+        w_bf = [tiles(sb, "w_bf%d_" % n, 1, [P, w, 4], BF16)[0] for n, w in enumerate(widths)]
+        w_codes = [tiles(sb, "w_codes%d_" % n, 1, [P, w], U32)[0] for n, w in enumerate(widths)]
+        w_scales = [tiles(sb, "w_scales%d_" % n, 1, [P, w], U8)[0] for n, w in enumerate(widths)]
+        squares = tiles(sb, "squares", 10, [P, 4, 128], BF16)
+        ssq = tiles(sb, "ssq", 10, [P, 4], F32)
+        rstd = tiles(sb, "rstd", 10, [P, 4], F32)
+        res = tiles(sb, "res", 10, [P, 4, 128], F32)
+        score = tiles(ps, "score", 4, [P, 512], F32)
         ybank = tiles(ps, "ybank", 4, [P, 4, 128], F32)
 
         def quantize(codes, scales, src):
@@ -71,11 +75,12 @@ def tile_rows_a_relu_kb_onorm_gate_kernel(tc, qT, kT, t, v, kb, gn, og, out):
         def runs(c):
             return ((0, 2, 4),) if c < 2 else ((0, 0, 2), (2, 6, 2))
 
-        def load_q(c):
+        def load_q(c, x):
             cols = slice(256 * (c % 2), 256 * (c % 2) + 256)
-            for g0, h0, nh in runs(c):
-                nc.sync.dma_start(out=q_raw[c][32 * g0 : 32 * (g0 + nh)],
-                                  in_=qT[h0 : h0 + nh, :, cols].rearrange("h (p j) n -> (h p) j n", j=4))
+            g0, h0, nh = runs(c)[x]
+            queue = nc.scalar if x else nc.sync
+            queue.dma_start(out=q_raw[c][32 * g0 : 32 * (g0 + nh)],
+                            in_=qT[h0 : h0 + nh, :, cols].rearrange("h (p j) n -> (h p) j n", j=4))
 
         def load_og(c):
             rows = slice(256 * (c % 2), 256 * (c % 2) + 256)
@@ -109,47 +114,55 @@ def tile_rows_a_relu_kb_onorm_gate_kernel(tc, qT, kT, t, v, kb, gn, og, out):
             nc.vector.tensor_tensor(tkb[:], tabs[:], kb_sb[:], ALU.mult)
 
         def ik(j):
-            cast("ik%d" % j, k_bf[:, :, 32 * j : 32 * j + 32, :].rearrange("p r s j -> p s r j"),
-                 k_raw[:, :, 128 * j : 128 * j + 128].rearrange("p j (s r) -> p s r j", r=4))
+            cast("ik%d" % j, k_bf[:, :, 32 * j : 32 * j + 32, :].rearrange("p r s j -> p s j r"),
+                 k_raw[:, :, 128 * j : 128 * j + 128].rearrange("p j (s r) -> p s j r", r=4))
 
         def zk(x):
             quantize(k_codes[:, 256 * x : 256 * x + 256], k_scales[:, 256 * x : 256 * x + 256],
                      k_bf[:, 2 * x : 2 * x + 2].rearrange("p r s j -> p (r s j)"))
 
         def iq(c, x):
-            cast("i" + QN[c] + "ab"[x], q_bf[c][:, :, 64 * x : 64 * x + 64, :].rearrange("p u m j -> p m u j"),
-                 q_raw[c][:, :, 128 * x : 128 * x + 128].rearrange("p j (m u) -> p m u j", u=2))
+            cast("i" + QN[c] + "ab"[x], q_bf[c][:, :, 64 * x : 64 * x + 64, :].rearrange("p u m j -> p m j u"),
+                 q_raw[c][:, :, 128 * x : 128 * x + 128].rearrange("p j (m u) -> p m j u", u=2))
 
         def zq(c):
             quantize(q_codes[c][:], q_scales[c][:], q_bf[c][:].rearrange("p u m j -> p (u m j)"))
 
         def iv():
-            nc.vector.tensor_tensor(v_bf[:], v_raw[:].rearrange("p k j e -> p k e j"),
-                                    sgn[:].unsqueeze(1).unsqueeze(1).broadcast_to([P, KV, 128, 4]), ALU.mult)
+            for k in range(KV):
+                nc.vector.tensor_tensor(v_bf[:, k].rearrange("p (c i) j -> p c j i", i=4),
+                                        v_raw[:, k].rearrange("p j (c i) -> p c j i", i=4),
+                                        sgn[:].unsqueeze(1).unsqueeze(3).broadcast_to([P, 32, 4, 4]), ALU.mult)
 
         def zv():
             quantize(v_codes[:], v_scales[:], v_bf[:].rearrange("p k e j -> p (k e j)"))
 
-        def mm(n, part):
-            g, c = n % 4, n // 4
+        def fill_rows(n, f):
+            per = 4 // len(UNITS[n][1])
+            return list(range(f * per, (f + 1) * per))
+
+        def mm(n, f):
+            g, blocks = UNITS[n]
             rows = slice(32 * g, 32 * g + 32)
-            for rr in range(2):
-                kc = slice(128 * (2 * part + rr), 128 * (2 * part + rr) + 128)
-                for u in range(2):
+            slot = 0
+            for r in fill_rows(n, f):
+                kc = slice(128 * r, 128 * r + 128)
+                for c, u in blocks:
                     qc = slice(128 * u, 128 * u + 128)
-                    nc.tensor.matmul_mx(out=score[g][:, rr, qc], lhsT=k_codes[rows, kc].bitcast(X4),
+                    nc.tensor.matmul_mx(out=score[g][:, 128 * slot : 128 * slot + 128], lhsT=k_codes[rows, kc].bitcast(X4),
                                         lhsT_scale=k_scales[rows, kc], rhs=q_codes[c][rows, qc].bitcast(X4),
                                         rhs_scale=q_scales[c][rows, qc], start=True, stop=True)
+                    slot += 1
 
-        def s1(n, part):
-            g = n % 4
-            for rr in range(2):
-                r = 2 * part + rr
-                if "s%s%d" % ("ab"[part], n) in ON_ACT:
-                    nc.scalar.activation(out=w_rows[n][:, r, :], in_=score[g][:, rr, :], func=ACT.Relu,
+        def s1(n, f):
+            g, w = UNITS[n][0], widths[n]
+            for i, r in enumerate(fill_rows(n, f)):
+                src = score[g][:, w * i : w * i + w]
+                if "s%d_%d" % (n, f) in ON_ACT:
+                    nc.scalar.activation(out=w_rows[n][:, r, :], in_=src, func=ACT.Relu,
                                          bias=tkb[:, r : r + 1], scale=tabs[:, r : r + 1])
                 else:
-                    nc.vector.tensor_scalar(w_rows[n][:, r, :], score[g][:, rr, :], kb_sb[:, r : r + 1],
+                    nc.vector.tensor_scalar(w_rows[n][:, r, :], src, kb_sb[:, r : r + 1],
                                             tabs[:, r : r + 1], ALU.add, ALU.mult)
 
         def iw(n):
@@ -163,12 +176,14 @@ def tile_rows_a_relu_kb_onorm_gate_kernel(tc, qT, kT, t, v, kb, gn, og, out):
         def zw(n):
             quantize(w_codes[n][:], w_scales[n][:], w_bf[n][:].rearrange("p q r -> p (q r)"))
 
-        def ymm(n):
-            kv = (n % 4) // 2
-            vc = slice(128 * kv, 128 * kv + 128)
-            for u in range(2):
-                qc = slice(128 * u, 128 * u + 128)
-                nc.tensor.matmul_mx(out=ybank[(n // 2) % 4][:, 2 * (n % 2) + u, :], lhsT=w_codes[n][:, qc].bitcast(X4),
+        def members(p):
+            return [(n, i, UNITS[n][0], c, u) for n in GROUPS[p] for i, (c, u) in enumerate(UNITS[n][1])]
+
+        def ymm(p):
+            for x, (n, i, g, c, u) in enumerate(members(p)):
+                vc = slice(128 * (g // 2), 128 * (g // 2) + 128)
+                qc = slice(128 * i, 128 * i + 128)
+                nc.tensor.matmul_mx(out=ybank[p % 4][:, x, :], lhsT=w_codes[n][:, qc].bitcast(X4),
                                     lhsT_scale=w_scales[n][:, qc], rhs=v_codes[:, vc].bitcast(X4),
                                     rhs_scale=v_scales[:, vc], start=True, stop=True)
 
@@ -177,36 +192,49 @@ def tile_rows_a_relu_kb_onorm_gate_kernel(tc, qT, kT, t, v, kb, gn, og, out):
 
         def g2(p):
             g0 = 2 * (p % 2)
-            nc.vector.tensor_tensor(gate[p][:], sig[p // 2][:, g0 : g0 + 2, :].rearrange("p g (u e) -> p (g u) e", u=2),
+            nc.vector.tensor_tensor(gate[p // 2][:, g0 : g0 + 2, :].rearrange("p g (u e) -> p (g u) e", u=2),
+                                    sig[p // 2][:, g0 : g0 + 2, :].rearrange("p g (u e) -> p (g u) e", u=2),
                                     gn_sb[:].unsqueeze(1).broadcast_to([P, 4, 128]), ALU.mult)
 
         def ss(p):
-            for i in range(4):
-                nc.scalar.activation(out=squares[p][:, i, :], in_=ybank[p % 4][:, i, :], func=ACT.Square,
-                                     accum_out=ssq[p][:, i : i + 1])
+            for x in range(len(members(p))):
+                nc.scalar.activation(out=squares[p][:, x, :], in_=ybank[p % 4][:, x, :], func=ACT.Square,
+                                     accum_out=ssq[p][:, x : x + 1])
 
         def rs(p):
-            nc.scalar.activation(out=rstd[p][:], in_=ssq[p][:], func=ACT.Abs_reciprocal_sqrt,
+            k = len(members(p))
+            nc.scalar.activation(out=rstd[p][:, :k], in_=ssq[p][:, :k], func=ACT.Abs_reciprocal_sqrt,
                                  scale=1.0 / 128.0, bias=256.0 * 1e-5)
 
         def fin(p):
-            for i in range(4):
-                nc.vector.scalar_tensor_tensor(res[p][:, i, :], ybank[p % 4][:, i, :], rstd[p][:, i : i + 1],
-                                               gate[p][:, i, :], ALU.mult, ALU.mult)
+            for x, (n, i, g, c, u) in enumerate(members(p)):
+                nc.vector.scalar_tensor_tensor(res[p][:, x, :], ybank[p % 4][:, x, :], rstd[p][:, x : x + 1],
+                                               gate[c][:, g, 128 * u : 128 * u + 128], ALU.mult, ALU.mult)
 
         def st(p):
-            c = p // 2
-            h0 = HEADS[c // 2][2 * (p % 2)]
-            rows = slice(256 * (c % 2), 256 * (c % 2) + 256)
-            nc.sync.dma_start(out=out[h0 : h0 + 2, rows, :].rearrange("h (m u) e -> m h (u e)", u=2),
-                              in_=res[p][:].rearrange("p (g u) e -> p g (u e)", u=2))
+            mem = members(p)
+            if len(GROUPS[p]) == 2:
+                n, i, g, c, u = mem[0]
+                h0 = HEADS[c // 2][g]
+                rows = slice(256 * (c % 2), 256 * (c % 2) + 256)
+                nc.sync.dma_start(out=out[h0 : h0 + 2, rows, :].rearrange("h (m u) e -> m h (u e)", u=2),
+                                  in_=res[p][:].rearrange("p (g u) e -> p g (u e)", u=2))
+                return
+            for x in range(0, len(mem), 2):
+                n, i, g, c, u = mem[x]
+                k = min(2, len(mem))
+                rows = slice(256 * (c % 2), 256 * (c % 2) + 256)
+                nc.sync.dma_start(out=out[HEADS[c // 2][g], rows, :].rearrange("(m u) e -> m u e", u=2)[:, u : u + k, :],
+                                  in_=res[p][:, x : x + k, :])
 
         def bind(f, *a):
             return lambda: f(*a)
 
         task = {"dt": dt, "dk": dk, "dv": dv, "cst": cst, "iv": iv, "zv": zv, "sw": lambda: None}
         for c in range(4):
-            task["d" + QN[c]] = bind(load_q, c)
+            task["d" + QN[c]] = bind(load_q, c, 0)
+            task["x" + QN[c]] = bind(load_q, c, 1)
+            task["h" + QN[c]] = task["sw"]
             task["dog%d" % c] = bind(load_og, c)
             task["ik%d" % c] = bind(ik, c)
             task["i" + QN[c] + "a"] = bind(iq, c, 0)
@@ -215,15 +243,16 @@ def tile_rows_a_relu_kb_onorm_gate_kernel(tc, qT, kT, t, v, kb, gn, og, out):
             task["sig%d" % c] = bind(sg, c)
         for x in range(2):
             task["zk%d" % x] = bind(zk, x)
-        for n in range(16):
-            for part in range(2):
-                task["m%s%d" % ("ab"[part], n)] = bind(mm, n, part)
-                task["s%s%d" % ("ab"[part], n)] = bind(s1, n, part)
+        for n in range(len(UNITS)):
+            for f in range(len(UNITS[n][1])):
+                task["m%d_%d" % (n, f)] = bind(mm, n, f)
+                task["s%d_%d" % (n, f)] = bind(s1, n, f)
             task["iw%d" % n] = bind(iw, n)
             task["zw%d" % n] = bind(zw, n)
-            task["y%d" % n] = bind(ymm, n)
         for p in range(8):
             task["g%d" % p] = bind(g2, p)
+        for p in range(len(GROUPS)):
+            task["y%d" % p] = bind(ymm, p)
             task["ss%d" % p] = bind(ss, p)
             task["rs%d" % p] = bind(rs, p)
             task["fin%d" % p] = bind(fin, p)

@@ -15,8 +15,8 @@ ACT = mybir.ActivationFunctionType
 
 P = 128
 HEADS = ((2, 3, 4, 5), (0, 1, 6, 7))
-ORDER = ["dk","dt","dqA0","ik0","dog0","ik2","ik3","ik1","zk0","iqA0a","xqB0","dv","iqA0b","zqA0","dqB0","zk1","cst","sig0","m0_0","m1_0","dqA1","iv","s0_0","m2_0","s1_0","m3_0","g0","s2_0","dog1","m0_1","iqB0a","m1_1","s3_0","zv","iqB0b","m2_1","s0_1","iqA1a","dog3","iqA1b","m3_1","s1_1","zqB0","zqA1","s2_1","xqB1","g1","dqB1","m4_0","sig1","iw0","m6_0","iw2","dog2","m5_0","s4_0","zw0","s3_1","g3","m4_1","s5_0","sig3","iw1","m5_1","s4_1","iqB1a","m7_0","zw2","sig2","s6_0","m4_2","s5_1","m6_1","s7_0","g2","s4_2","m5_2","iw3","s6_1","m7_1","zw1","iqB1b","sw","m4_3","s5_2","g4","m5_3","zw3","s4_3","zqB1","m6_2","g5","s7_1","y1","iw4","s5_3","m7_2","s6_2","m9_0","g6","ss1","m6_3","iw5","s7_2","y0","rs1","s9_0","m7_3","zw4","s6_3","m8_0","zw5","ss0","m9_1","fin1","st1","s7_3","y2","iw6","rs0","s8_0","m10_0","ss2","y3","fin0","st0","m8_1","s10_0","zw6","m11_0","s9_1","iw7","y4","s8_1","m10_1","ss3","iw9","zw7","ss4","iw8","rs2","s10_1","y5","zw9","s11_0","fin2","st2","zw8","rs4","rs3","iw11","iw10","m12_0","ss5","fin4","st4","y6","zw11","s12_0","fin3","st3","y8","rs5","zw10","ss6","iw12","y7","fin5","st5","ss8","rs6","zw12","fin6","st6","ss7","y9","g7","rs7","rs8","ss9","fin7","st7","rs9","fin8","st8","fin9","st9"]
-ON_ACT = ["ik2","iqA0a","s0_0","s1_0","s2_0","s3_0","s0_1","s1_1","s2_1","s4_0","s3_1","s4_1","s7_0","s4_2","s6_1","s4_3","s7_1","s5_3","s6_2","s7_2","s9_0","s6_3","s7_3","s8_0","s10_0","s9_1","s8_1","s10_1","s11_0","iw11","s12_0"]
+ORDER = ["dk","dt","dqA0","dog0","ikb","ika","dqA1","iqA0b","iqA0a","zk0","xqB0","zqA0","dqB0","zk1","sig0","m0_0","cst","m1_0","dv","s0_0","iqA1","m2_0","s1_0","g0","m0_1","dog1","s2_0","m1_1","iqB0","xqB1","s0_1","m2_1","dqB1","zqA1","s1_1","m3_0","zqB0","iv","s2_1","m4_0","dog2","s3_0","m5_0","iw0","m6_0","s4_0","dog3","s5_0","m3_1","sig1","zw0","m4_1","s6_0","m5_1","s3_1","iqB1","s4_1","m7_0","s5_1","sig2","m6_1","iw1","m4_2","s7_0","iw2","m5_2","s6_1","zw1","m7_1","zv","s4_2","zqB1","zw2","s5_2","g1","m4_3","s7_1","y0","s4_3","iw3","m5_3","sig3","m6_2","g2","m7_2","s5_3","m8_0","g3","s6_2","m9_0","s7_2","zw3","m6_3","iw4","ss0","m7_3","s8_0","iw5","s6_3","m8_1","s7_3","y1","zw4","s9_0","m10_0","zw5","s8_1","y2","iw6","ss1","m11_0","m9_1","s10_0","iw7","m10_1","y3","iw8","rs0","zw6","rs1","s10_1","fin0","st0","s11_0","fin1","st1","s9_1","m12_0","zw7","ss2","y4","zw8","y5","ss3","iw9","iw10","rs2","rs3","ss4","iw11","fin2","st2","s12_0","zw9","ss5","zw10","y6","zw11","fin3","st3","rs4","rs5","iw12","fin4","st4","ss6","y7","fin5","st5","y8","rs6","ss7","zw12","fin6","st6","ss8","y9","rs7","rs8","fin7","st7","ss9","fin8","st8","rs9","fin9","st9"]
+ON_ACT = ["s0_0","s0_1","s1_0","s1_1","s2_0","s2_1","s3_0","s3_1","s4_0","s4_1","s4_2","s4_3","s5_2","s5_3","s6_1","s6_2","s6_3","s7_0","s7_1","s7_2","s7_3","s8_0","s8_1","s9_0","s9_1","s10_0","s10_1","s11_0","s12_0","iw12","ika","iqA0a"]
 UNITS = ([(g, [(0, 0), (0, 1)]) for g in range(4)] + [(g, [(1, 0), (1, 1), (2, 0), (2, 1)]) for g in range(4)]
          + [(g, [(3, 0), (3, 1)]) for g in range(3)] + [(3, [(3, 0)]), (3, [(3, 1)])])
 GROUPS = [[0, 1], [2, 3], [4], [5], [6], [7], [8, 9], [10], [11], [12]]
@@ -113,17 +113,17 @@ def tile_rows_a_relu_kb_onorm_gate_kernel(tc, qT, kT, t, v, kb, gn, og, out):
             nc.vector.tensor_tensor(tabs[:], t_sb[:], sgn[:], ALU.mult)
             nc.vector.tensor_tensor(tkb[:], tabs[:], kb_sb[:], ALU.mult)
 
-        def ik(j):
-            cast("ik%d" % j, k_bf[:, :, 32 * j : 32 * j + 32, :].rearrange("p r s j -> p s j r"),
-                 k_raw[:, :, 128 * j : 128 * j + 128].rearrange("p j (s r) -> p s j r", r=4))
+        def ik(name, a, b):
+            cast(name, k_bf[:, :, a:b, :].rearrange("p r s j -> p s j r"),
+                 k_raw[:, :, 4 * a : 4 * b].rearrange("p j (s r) -> p s j r", r=4))
 
         def zk(x):
             quantize(k_codes[:, 256 * x : 256 * x + 256], k_scales[:, 256 * x : 256 * x + 256],
                      k_bf[:, 2 * x : 2 * x + 2].rearrange("p r s j -> p (r s j)"))
 
-        def iq(c, x):
-            cast("i" + QN[c] + "ab"[x], q_bf[c][:, :, 64 * x : 64 * x + 64, :].rearrange("p u m j -> p m j u"),
-                 q_raw[c][:, :, 128 * x : 128 * x + 128].rearrange("p j (m u) -> p m j u", u=2))
+        def iq(name, c, a, b):
+            cast(name, q_bf[c][:, :, a:b, :].rearrange("p u m j -> p m j u"),
+                 q_raw[c][:, :, 2 * a : 2 * b].rearrange("p j (m u) -> p m j u", u=2))
 
         def zq(c):
             quantize(q_codes[c][:], q_scales[c][:], q_bf[c][:].rearrange("p u m j -> p (u m j)"))
@@ -166,10 +166,12 @@ def tile_rows_a_relu_kb_onorm_gate_kernel(tc, qT, kT, t, v, kb, gn, og, out):
                                             tabs[:, r : r + 1], ALU.add, ALU.mult)
 
         def iw(n):
-            dst = w_bf[n][:].rearrange("p (c i) r -> p c r i", i=4)
-            src = w_rows[n][:].rearrange("p r (c i) -> p c r i", i=4)
+            dst = w_bf[n][:]
+            src = w_rows[n][:].rearrange("p r q -> p q r")
             if "iw%d" % n in ON_ACT:
                 nc.scalar.activation(out=dst, in_=src, func=ACT.Relu)
+            elif all("s%d_%d" % (n, f) in ON_ACT for f in range(len(UNITS[n][1]))):
+                nc.vector.tensor_copy(out=dst, in_=src)
             else:
                 nc.vector.tensor_scalar(dst, src, 0.0, None, ALU.max)
 
@@ -190,11 +192,10 @@ def tile_rows_a_relu_kb_onorm_gate_kernel(tc, qT, kT, t, v, kb, gn, og, out):
         def sg(c):
             nc.scalar.activation(out=sig[c][:], in_=og_sb[c][:], func=ACT.Sigmoid)
 
-        def g2(p):
-            g0 = 2 * (p % 2)
-            nc.vector.tensor_tensor(gate[p // 2][:, g0 : g0 + 2, :].rearrange("p g (u e) -> p (g u) e", u=2),
-                                    sig[p // 2][:, g0 : g0 + 2, :].rearrange("p g (u e) -> p (g u) e", u=2),
-                                    gn_sb[:].unsqueeze(1).broadcast_to([P, 4, 128]), ALU.mult)
+        def g2(c):
+            nc.vector.tensor_tensor(gate[c][:].rearrange("p g (u e) -> p (g u) e", u=2),
+                                    sig[c][:].rearrange("p g (u e) -> p (g u) e", u=2),
+                                    gn_sb[:].unsqueeze(1).broadcast_to([P, 8, 128]), ALU.mult)
 
         def ss(p):
             for x in range(len(members(p))):
@@ -236,9 +237,8 @@ def tile_rows_a_relu_kb_onorm_gate_kernel(tc, qT, kT, t, v, kb, gn, og, out):
             task["x" + QN[c]] = bind(load_q, c, 1)
             task["h" + QN[c]] = task["sw"]
             task["dog%d" % c] = bind(load_og, c)
-            task["ik%d" % c] = bind(ik, c)
-            task["i" + QN[c] + "a"] = bind(iq, c, 0)
-            task["i" + QN[c] + "b"] = bind(iq, c, 1)
+            task["i" + QN[c]] = bind(iq, "i" + QN[c], c, 0, 128)
+            task["g%d" % c] = bind(g2, c)
             task["z" + QN[c]] = bind(zq, c)
             task["sig%d" % c] = bind(sg, c)
         for x in range(2):
@@ -249,8 +249,10 @@ def tile_rows_a_relu_kb_onorm_gate_kernel(tc, qT, kT, t, v, kb, gn, og, out):
                 task["s%d_%d" % (n, f)] = bind(s1, n, f)
             task["iw%d" % n] = bind(iw, n)
             task["zw%d" % n] = bind(zw, n)
-        for p in range(8):
-            task["g%d" % p] = bind(g2, p)
+        task["ika"] = bind(ik, "ika", 0, 44)
+        task["ikb"] = bind(ik, "ikb", 44, 128)
+        task["iqA0a"] = bind(iq, "iqA0a", 0, 0, 44)
+        task["iqA0b"] = bind(iq, "iqA0b", 0, 44, 128)
         for p in range(len(GROUPS)):
             task["y%d" % p] = bind(ymm, p)
             task["ss%d" % p] = bind(ss, p)

from contextlib import ExitStack

import concourse.mybir as mybir

H, KV, D, NQ, N = 8, 2, 128, 512, 512
FLOPS = 2 * 2 * H * NQ * N * D

F32 = mybir.dt.float32
BF16 = mybir.dt.bfloat16
U32 = mybir.dt.uint32
U8 = mybir.dt.uint8
X4 = mybir.dt.float8_e4m3fn_x4
ALU = mybir.AluOpType
ACT = mybir.ActivationFunctionType

P = 128
HEADS = ((2, 3, 4, 5), (0, 1, 6, 7))
ORDER = ["dk","dt","dqA0","dog0","ikb","ika","dqA1","iqA0b","iqA0a","zk0","xqB0","zqA0","dqB0","zk1","sig0","m0_0","cst","m1_0","dv","s0_0","iqA1","m2_0","s1_0","g0","m0_1","dog1","s2_0","m1_1","iqB0","xqB1","s0_1","m2_1","dqB1","zqA1","s1_1","m3_0","zqB0","iv","s2_1","m4_0","dog2","s3_0","m5_0","iw0","m6_0","s4_0","dog3","s5_0","m3_1","sig1","zw0","m4_1","s6_0","m5_1","s3_1","iqB1","s4_1","m7_0","s5_1","sig2","m6_1","iw1","m4_2","s7_0","iw2","m5_2","s6_1","zw1","m7_1","zv","s4_2","zqB1","zw2","s5_2","g1","m4_3","s7_1","y0","s4_3","iw3","m5_3","sig3","m6_2","g2","m7_2","s5_3","m8_0","g3","s6_2","m9_0","s7_2","zw3","m6_3","iw4","ss0","m7_3","s8_0","iw5","s6_3","m8_1","s7_3","y1","zw4","s9_0","m10_0","zw5","s8_1","y2","iw6","ss1","m11_0","m9_1","s10_0","iw7","m10_1","y3","iw8","rs0","zw6","rs1","s10_1","fin0","st0","s11_0","fin1","st1","s9_1","m12_0","zw7","ss2","y4","zw8","y5","ss3","iw9","iw10","rs2","rs3","ss4","iw11","fin2","st2","s12_0","zw9","ss5","zw10","y6","zw11","fin3","st3","rs4","rs5","iw12","fin4","st4","ss6","y7","fin5","st5","y8","rs6","ss7","zw12","fin6","st6","ss8","y9","rs7","rs8","fin7","st7","ss9","fin8","st8","rs9","fin9","st9"]
ON_ACT = ["s0_0","s0_1","s1_0","s1_1","s2_0","s2_1","s3_0","s3_1","s4_0","s4_1","s4_2","s4_3","s5_2","s5_3","s6_1","s6_2","s6_3","s7_0","s7_1","s7_2","s7_3","s8_0","s8_1","s9_0","s9_1","s10_0","s10_1","s11_0","s12_0","iw12","ika","iqA0a"]
UNITS = ([(g, [(0, 0), (0, 1)]) for g in range(4)] + [(g, [(1, 0), (1, 1), (2, 0), (2, 1)]) for g in range(4)]
         + [(g, [(3, 0), (3, 1)]) for g in range(3)] + [(3, [(3, 0)]), (3, [(3, 1)])])
GROUPS = [[0, 1], [2, 3], [4], [5], [6], [7], [8, 9], [10], [11], [12]]


def tile_rows_a_relu_kb_onorm_gate_kernel(tc, qT, kT, t, v, kb, gn, og, out):
    nc = tc.nc
    with ExitStack() as ctx:
        sb = ctx.enter_context(tc.tile_pool(name="sb", bufs=1))
        ps = ctx.enter_context(tc.psum_pool(name="ps", bufs=1))

        def tiles(pool, name, count, shape, dtype):
            if pool is ps:
                return [pool.tile(shape, dtype, name="%s%d" % (name, i)) for i in range(count)]
            return [pool.tile(shape, dtype, name="%s%d" % (name, i), align_bytes=64) for i in range(count)]

        (t_sb, kb_sb, sgn, tabs, tkb, ge0) = tiles(sb, "tok", 6, [P, 4], F32)
        (warm_in, warm_out) = tiles(sb, "warm", 2, [P, 1], F32)
        (gn_sb,) = tiles(sb, "gn", 1, [P, 128], F32)
        (k_raw,) = tiles(sb, "k_raw", 1, [P, 4, N], F32)
        (k_bf,) = tiles(sb, "k_bf", 1, [P, 4, 128, 4], BF16)
        (k_codes,) = tiles(sb, "k_codes", 1, [P, N], U32)
        (k_scales,) = tiles(sb, "k_scales", 1, [P, N], U8)
        (v_raw,) = tiles(sb, "v_raw", 1, [P, KV, 4, 128], F32)
        (v_bf,) = tiles(sb, "v_bf", 1, [P, KV, 128, 4], BF16)
        (v_codes,) = tiles(sb, "v_codes", 1, [P, KV * 128], U32)
        (v_scales,) = tiles(sb, "v_scales", 1, [P, KV * 128], U8)
        q_raw = tiles(sb, "q_raw", 4, [P, 4, 256], F32)
        q_bf = tiles(sb, "q_bf", 4, [P, 2, 128, 4], BF16)
        q_codes = tiles(sb, "q_codes", 4, [P, 256], U32)
        q_scales = tiles(sb, "q_scales", 4, [P, 256], U8)
        og_sb = tiles(sb, "og_sb", 4, [P, 4, 256], F32)
        sig = tiles(sb, "sig", 4, [P, 4, 256], F32)
        gate = tiles(sb, "gate", 4, [P, 4, 256], F32)
        widths = [128 * len(blocks) for g, blocks in UNITS]
        w_rows = [tiles(sb, "w_rows%d_" % n, 1, [P, 4, w], BF16)[0] for n, w in enumerate(widths)]
        w_bf = [tiles(sb, "w_bf%d_" % n, 1, [P, w, 4], BF16)[0] for n, w in enumerate(widths)]
        w_codes = [tiles(sb, "w_codes%d_" % n, 1, [P, w], U32)[0] for n, w in enumerate(widths)]
        w_scales = [tiles(sb, "w_scales%d_" % n, 1, [P, w], U8)[0] for n, w in enumerate(widths)]
        squares = tiles(sb, "squares", 10, [P, 4, 128], BF16)
        ssq = tiles(sb, "ssq", 10, [P, 4], F32)
        rstd = tiles(sb, "rstd", 10, [P, 4], F32)
        res = tiles(sb, "res", 10, [P, 4, 128], F32)
        score = tiles(ps, "score", 4, [P, 512], F32)
        ybank = tiles(ps, "ybank", 4, [P, 4, 128], F32)

        def quantize(codes, scales, src):
            nc.vector.quantize_mx(out=codes.bitcast(X4), scales=scales, in_=src)

        def cast(name, dst, src):
            if name in ON_ACT:
                nc.scalar.copy(out=dst, in_=src)
            else:
                nc.vector.tensor_copy(out=dst, in_=src)

        def runs(c):
            return ((0, 2, 4),) if c < 2 else ((0, 0, 2), (2, 6, 2))

        def load_q(c, x):
            cols = slice(256 * (c % 2), 256 * (c % 2) + 256)
            g0, h0, nh = runs(c)[x]
            queue = nc.scalar if x else nc.sync
            queue.dma_start(out=q_raw[c][32 * g0 : 32 * (g0 + nh)],
                            in_=qT[h0 : h0 + nh, :, cols].rearrange("h (p j) n -> (h p) j n", j=4))

        def load_og(c):
            rows = slice(256 * (c % 2), 256 * (c % 2) + 256)
            for g0, h0, nh in runs(c):
                nc.sync.dma_start(out=og_sb[c][:, g0 : g0 + nh, :],
                                  in_=og[h0 : h0 + nh, rows, :].rearrange("h (m u) e -> m h (u e)", u=2))

        QN = ("qA0", "qA1", "qB0", "qB1")

        def dt():
            nc.scalar.dma_start(out=t_sb[:], in_=t.rearrange("(p r) o -> p (r o)", r=4))
            nc.scalar.dma_start(out=kb_sb[:], in_=kb.rearrange("(p r) o -> p (r o)", r=4))
            nc.scalar.dma_start(out=gn_sb[:], in_=gn)
            nc.vector.memset(warm_in[:], 0.0)
            nc.scalar.activation(out=warm_out[:], in_=warm_in[:], func=ACT.Sigmoid)

        def dk():
            rows = kT.rearrange("k (p j) n -> (k p) j n", j=4)
            nc.sync.dma_start(out=k_raw[32:96], in_=rows)
            nc.scalar.dma_start(out=k_raw[96:128], in_=rows[32:64])
            nc.sync.dma_start(out=k_raw[0:32], in_=rows[0:32])

        def dv():
            nc.sync.dma_start(out=v_raw[:].rearrange("p k j e -> p k (j e)"),
                              in_=v.rearrange("k (p j) e -> p k (j e)", j=4))

        def cst():
            nc.vector.tensor_scalar(ge0[:], t_sb[:], 0.0, 2.0, ALU.is_ge, ALU.mult)
            nc.vector.tensor_scalar(sgn[:], ge0[:], -1.0, None, ALU.add)
            nc.vector.tensor_tensor(tabs[:], t_sb[:], sgn[:], ALU.mult)
            nc.vector.tensor_tensor(tkb[:], tabs[:], kb_sb[:], ALU.mult)

        def ik(name, a, b):
            cast(name, k_bf[:, :, a:b, :].rearrange("p r s j -> p s j r"),
                 k_raw[:, :, 4 * a : 4 * b].rearrange("p j (s r) -> p s j r", r=4))

        def zk(x):
            quantize(k_codes[:, 256 * x : 256 * x + 256], k_scales[:, 256 * x : 256 * x + 256],
                     k_bf[:, 2 * x : 2 * x + 2].rearrange("p r s j -> p (r s j)"))

        def iq(name, c, a, b):
            cast(name, q_bf[c][:, :, a:b, :].rearrange("p u m j -> p m j u"),
                 q_raw[c][:, :, 2 * a : 2 * b].rearrange("p j (m u) -> p m j u", u=2))

        def zq(c):
            quantize(q_codes[c][:], q_scales[c][:], q_bf[c][:].rearrange("p u m j -> p (u m j)"))

        def iv():
            for k in range(KV):
                nc.vector.tensor_tensor(v_bf[:, k].rearrange("p (c i) j -> p c j i", i=4),
                                        v_raw[:, k].rearrange("p j (c i) -> p c j i", i=4),
                                        sgn[:].unsqueeze(1).unsqueeze(3).broadcast_to([P, 32, 4, 4]), ALU.mult)

        def zv():
            quantize(v_codes[:], v_scales[:], v_bf[:].rearrange("p k e j -> p (k e j)"))

        def fill_rows(n, f):
            per = 4 // len(UNITS[n][1])
            return list(range(f * per, (f + 1) * per))

        def mm(n, f):
            g, blocks = UNITS[n]
            rows = slice(32 * g, 32 * g + 32)
            slot = 0
            for r in fill_rows(n, f):
                kc = slice(128 * r, 128 * r + 128)
                for c, u in blocks:
                    qc = slice(128 * u, 128 * u + 128)
                    nc.tensor.matmul_mx(out=score[g][:, 128 * slot : 128 * slot + 128], lhsT=k_codes[rows, kc].bitcast(X4),
                                        lhsT_scale=k_scales[rows, kc], rhs=q_codes[c][rows, qc].bitcast(X4),
                                        rhs_scale=q_scales[c][rows, qc], start=True, stop=True)
                    slot += 1

        def s1(n, f):
            g, w = UNITS[n][0], widths[n]
            for i, r in enumerate(fill_rows(n, f)):
                src = score[g][:, w * i : w * i + w]
                if "s%d_%d" % (n, f) in ON_ACT:
                    nc.scalar.activation(out=w_rows[n][:, r, :], in_=src, func=ACT.Relu,
                                         bias=tkb[:, r : r + 1], scale=tabs[:, r : r + 1])
                else:
                    nc.vector.tensor_scalar(w_rows[n][:, r, :], src, kb_sb[:, r : r + 1],
                                            tabs[:, r : r + 1], ALU.add, ALU.mult)

        def iw(n):
            dst = w_bf[n][:]
            src = w_rows[n][:].rearrange("p r q -> p q r")
            if "iw%d" % n in ON_ACT:
                nc.scalar.activation(out=dst, in_=src, func=ACT.Relu)
            elif all("s%d_%d" % (n, f) in ON_ACT for f in range(len(UNITS[n][1]))):
                nc.vector.tensor_copy(out=dst, in_=src)
            else:
                nc.vector.tensor_scalar(dst, src, 0.0, None, ALU.max)

        def zw(n):
            quantize(w_codes[n][:], w_scales[n][:], w_bf[n][:].rearrange("p q r -> p (q r)"))

        def members(p):
            return [(n, i, UNITS[n][0], c, u) for n in GROUPS[p] for i, (c, u) in enumerate(UNITS[n][1])]

        def ymm(p):
            for x, (n, i, g, c, u) in enumerate(members(p)):
                vc = slice(128 * (g // 2), 128 * (g // 2) + 128)
                qc = slice(128 * i, 128 * i + 128)
                nc.tensor.matmul_mx(out=ybank[p % 4][:, x, :], lhsT=w_codes[n][:, qc].bitcast(X4),
                                    lhsT_scale=w_scales[n][:, qc], rhs=v_codes[:, vc].bitcast(X4),
                                    rhs_scale=v_scales[:, vc], start=True, stop=True)

        def sg(c):
            nc.scalar.activation(out=sig[c][:], in_=og_sb[c][:], func=ACT.Sigmoid)

        def g2(c):
            nc.vector.tensor_tensor(gate[c][:].rearrange("p g (u e) -> p (g u) e", u=2),
                                    sig[c][:].rearrange("p g (u e) -> p (g u) e", u=2),
                                    gn_sb[:].unsqueeze(1).broadcast_to([P, 8, 128]), ALU.mult)

        def ss(p):
            for x in range(len(members(p))):
                nc.scalar.activation(out=squares[p][:, x, :], in_=ybank[p % 4][:, x, :], func=ACT.Square,
                                     accum_out=ssq[p][:, x : x + 1])

        def rs(p):
            k = len(members(p))
            nc.scalar.activation(out=rstd[p][:, :k], in_=ssq[p][:, :k], func=ACT.Abs_reciprocal_sqrt,
                                 scale=1.0 / 128.0, bias=256.0 * 1e-5)

        def fin(p):
            for x, (n, i, g, c, u) in enumerate(members(p)):
                nc.vector.scalar_tensor_tensor(res[p][:, x, :], ybank[p % 4][:, x, :], rstd[p][:, x : x + 1],
                                               gate[c][:, g, 128 * u : 128 * u + 128], ALU.mult, ALU.mult)

        def st(p):
            mem = members(p)
            if len(GROUPS[p]) == 2:
                n, i, g, c, u = mem[0]
                h0 = HEADS[c // 2][g]
                rows = slice(256 * (c % 2), 256 * (c % 2) + 256)
                nc.sync.dma_start(out=out[h0 : h0 + 2, rows, :].rearrange("h (m u) e -> m h (u e)", u=2),
                                  in_=res[p][:].rearrange("p (g u) e -> p g (u e)", u=2))
                return
            for x in range(0, len(mem), 2):
                n, i, g, c, u = mem[x]
                k = min(2, len(mem))
                rows = slice(256 * (c % 2), 256 * (c % 2) + 256)
                nc.sync.dma_start(out=out[HEADS[c // 2][g], rows, :].rearrange("(m u) e -> m u e", u=2)[:, u : u + k, :],
                                  in_=res[p][:, x : x + k, :])

        def bind(f, *a):
            return lambda: f(*a)

        task = {"dt": dt, "dk": dk, "dv": dv, "cst": cst, "iv": iv, "zv": zv, "sw": lambda: None}
        for c in range(4):
            task["d" + QN[c]] = bind(load_q, c, 0)
            task["x" + QN[c]] = bind(load_q, c, 1)
            task["h" + QN[c]] = task["sw"]
            task["dog%d" % c] = bind(load_og, c)
            task["i" + QN[c]] = bind(iq, "i" + QN[c], c, 0, 128)
            task["g%d" % c] = bind(g2, c)
            task["z" + QN[c]] = bind(zq, c)
            task["sig%d" % c] = bind(sg, c)
        for x in range(2):
            task["zk%d" % x] = bind(zk, x)
        for n in range(len(UNITS)):
            for f in range(len(UNITS[n][1])):
                task["m%d_%d" % (n, f)] = bind(mm, n, f)
                task["s%d_%d" % (n, f)] = bind(s1, n, f)
            task["iw%d" % n] = bind(iw, n)
            task["zw%d" % n] = bind(zw, n)
        task["ika"] = bind(ik, "ika", 0, 44)
        task["ikb"] = bind(ik, "ikb", 44, 128)
        task["iqA0a"] = bind(iq, "iqA0a", 0, 0, 44)
        task["iqA0b"] = bind(iq, "iqA0b", 0, 44, 128)
        for p in range(len(GROUPS)):
            task["y%d" % p] = bind(ymm, p)
            task["ss%d" % p] = bind(ss, p)
            task["rs%d" % p] = bind(rs, p)
            task["fin%d" % p] = bind(fin, p)
            task["st%d" % p] = bind(st, p)
        with tc.manual_schedule():
            for name in ORDER:
                task[name]()
